import numpy as np
import ml_dtypes


def mxq(x, axis, fmt="e4m3"):
    dtype, down = {"e4m3": (ml_dtypes.float8_e4m3fn, 7), "e5m2": (ml_dtypes.float8_e5m2, 14)}[fmt]
    v = np.moveaxis(np.asarray(x, np.float32).astype(ml_dtypes.bfloat16).astype(np.float64), axis, -1)
    blocks = v.reshape(v.shape[:-1] + (-1, 32))
    amax = np.abs(blocks).max(-1, keepdims=True)
    byte = np.maximum(np.where(amax > 0, np.frexp(amax)[1] - 1 + 127, 0) - down, 1)
    scale = np.exp2(byte - 127.0)
    codes = (blocks / scale).astype(np.float32).astype(dtype).astype(np.float64)
    return np.moveaxis((codes * scale).reshape(v.shape), -1, axis)


WIDE = False


def mx_kscale(k):
    if not WIDE:
        return np.ones(k)
    levels = np.array([10, -10, 5, -5, 0])
    if k % 512:
        return np.exp2(np.random.permutation(np.resize(levels, k // 32))).repeat(32)
    a = np.empty((k // 512, 16))
    for p in range(k // 512):
        a[p, :8] = np.random.permutation(np.resize(levels, 8))
        for g in range(8):
            far = levels[np.abs(levels - a[p, g]) >= 10]
            a[p, g + 8] = far[np.random.randint(len(far))]
    return np.exp2(a.ravel()).repeat(32)


def f64(x):
    return np.asarray(x).astype(np.float64)


def striped(idx):
    return np.tile(idx.reshape(-1, 16).T, (8, 1)).astype(np.uint16)


def unstriped(offs):
    return offs[:16].T.reshape(-1).astype(np.int64)


def pack_weight(w):
    k, n = w.shape
    w = f64(np.asarray(w, np.float32).astype(ml_dtypes.bfloat16)).reshape(k // 32, 32, n)
    amax = np.abs(w).max(1)
    byte = np.clip(np.where(amax > 0, np.frexp(amax)[1] - 1 + 127 - 7, 1), 1, 254)
    scaled = (w * np.exp2(127.0 - byte)[:, None, :]).reshape(k, n).astype(np.float32)
    words = np.ascontiguousarray(scaled.reshape(k // 512, 128, 4, n).transpose(0, 1, 3, 2)).astype(ml_dtypes.float8_e4m3fn).view(np.uint8)
    return words, np.ascontiguousarray(byte.astype(np.uint8).reshape(k // 512, 16, n))


def unpack_weight(words, scales):
    g, p, n, _ = words.shape
    vals = np.ascontiguousarray(words).view(ml_dtypes.float8_e4m3fn).astype(np.float64) * np.repeat(np.exp2(scales.astype(np.float64) - 127.0), 8, axis=1)[..., None]
    return vals.transpose(0, 1, 3, 2).reshape(g * 512, n)


K, T, S, N, H, U = 1024, 1024, 512, 128, 512, 1024


def setup_inputs():
    n = np.random.standard_normal
    s = mx_kscale(K)[:, None]
    u = mx_kscale(H)
    packed_xT = pack_weight(n((K, T)) * s)
    return {
        "x_words": packed_xT[0],
        "x_scales": packed_xT[1],
        "w1": (n((K, H)) / np.sqrt(K) / s).astype(np.float32),
        "w2": (n((K, H)) / np.sqrt(K) / s).astype(np.float32),
        "om": (np.random.uniform(0.2, 0.8, (H, U))).astype(np.float32),
        "unit": (np.random.uniform(0.6, 1.4, (H, 1)) * u[:, None]).astype(np.float32),
        "w3": (n((H, N)) / np.sqrt(H) / u[:, None]).astype(np.float32),
        "offs": striped(np.random.permutation(T)[:S]),
        "ta": striped(np.random.permutation(np.concatenate([np.arange(S), np.random.randint(0, S, U - S)]))),
        "tb": striped(np.random.permutation(np.concatenate([np.arange(S), np.random.randint(0, S, U - S)]))),
    }


def reference(x_words, x_scales, w1, w2, om, unit, w3, offs, ta, tb):
    xq = unpack_weight(x_words, x_scales)[:, unstriped(offs)]
    ys = mxq(f64(w2), 0, "e4m3").T @ xq
    prec = 0.8 * (np.log(np.exp(ys) + 1.0)) + 0.4
    pra = prec[:, unstriped(ta)]
    pa = f64(om) * pra
    y = mxq(f64(w1), 0, "e4m3").T @ xq
    ya = y[:, unstriped(ta)]
    prb = prec[:, unstriped(tb)]
    pb = (-1.0 * f64(om) + 1.0) * prb
    yb = y[:, unstriped(tb)]
    pf = pa + pb
    mf = (pa * ya + pb * yb) / pf
    hid = f64(unit) * mf
    return mxq(f64(w3), 0, "e4m3").T @ mxq(hid, 0, "e4m3")

@@ -1,0 +1,269 @@
+import math
+from contextlib import ExitStack
+
+import concourse.mybir as mybir
+from concourse.masks import make_identity
+
+K, T, S, N, H, U = 1024, 1024, 512, 128, 512, 1024
+FLOPS = 2 * (2 * K * H * S + H * N * U)
+
+F32 = mybir.dt.float32
+BF16 = mybir.dt.bfloat16
+I32 = mybir.dt.int32
+U32 = mybir.dt.uint32
+U16 = mybir.dt.uint16
+U8 = mybir.dt.uint8
+FP8X4 = mybir.dt.float8_e4m3fn_x4
+ALU = mybir.AluOpType
+ACT = mybir.ActivationFunctionType
+
+P = 128
+PACK = 4
+K_PASS = P * PACK
+PASSES = K // K_PASS
+ROW_TILES = H // P
+CHUNK = 256
+CHUNKS = U // CHUNK
+BLOCKS = CHUNK // P
+LIST_ROWS = 16
+OM_COLS = 512
+
+
+def tile_picked_ycovin_mean_p_kernel(
+    tc, x_words, x_scales, w1, w2, om, unit, w3, offs, ta, tb, out
+):
+    nc = tc.nc
+    with ExitStack() as ctx:
+        keep = ctx.enter_context(tc.tile_pool(name="keep", bufs=1))
+        work = ctx.enter_context(tc.tile_pool(name="work", bufs=3))
+        psum = ctx.enter_context(tc.psum_pool(name="psum", bufs=8))
+
+        def load_rows(name, rows):
+            raw = keep.tile([P, PACK, rows.shape[1]], F32, name=name + "_raw")
+            nc.sync.dma_start(out=raw[:], in_=rows.rearrange("(p j) c -> p j c", j=PACK))
+            return raw
+
+        def round_and_interleave(name, raw, copy):
+            grouped = keep.tile([P, raw.shape[2], PACK], BF16, name=name + "_bf16", align_bytes=64)
+            copy(
+                out=grouped[:].rearrange("p (c i) j -> p c j i", i=4),
+                in_=raw[:].rearrange("p j (c i) -> p c j i", i=4),
+            )
+            return grouped
+
+        def quantize(pool, name, grouped):
+            width = grouped.shape[1]
+            codes = pool.tile([P, width], U32, name=name + "_codes", align_bytes=64)
+            scales = pool.tile([P, width], U8, name=name + "_scales", align_bytes=64)
+            nc.vector.quantize_mx(
+                out=codes[:].bitcast(FP8X4), scales=scales[:], in_=grouped[:].rearrange("p c j -> p (c j)")
+            )
+            return codes, scales
+
+        def bank(name):
+            return psum.tile([P, 512], F32, name=name, tag="bank")
+
+        scale_table = keep.tile([P, T], U8, name="scale_table", align_bytes=64)
+        nc.gpsimd.memset(scale_table[:], 0)
+        ident = keep.tile([P, P], F32, name="ident")
+        make_identity(nc, ident[:])
+
+        half = H // 2
+        w2_raw = [[load_rows("w2_0", w2[0:K_PASS, :])]]
+        offs_sb = keep.tile([P, S // LIST_ROWS], U16, name="offs_sb")
+        nc.sync.dma_start(offs_sb[:], offs)
+        word_tables = []
+        for o in range(PASSES):
+            table = keep.tile([P, T], U32, name=f"word_table{o}", align_bytes=64)
+            nc.sync.dma_start(out=table[:].bitcast(I32), in_=x_words[o].rearrange("p n t -> p (n t)").bitcast(I32))
+            word_tables.append(table)
+        for q in range(4):
+            nc.sync.dma_start(
+                out=scale_table[32 * q : 32 * q + 4 * PASSES, :].bitcast(I32),
+                in_=x_scales.bitcast(I32)[:, 4 * q : 4 * q + 4, :],
+            )
+        w2_raw.append([load_rows(f"w2_1{h}", w2[K_PASS:K, h * half : (h + 1) * half]) for h in range(2)])
+        w1_raw = [load_rows(f"w1_{o}", w1[o * K_PASS : (o + 1) * K_PASS, :]) for o in range(PASSES)]
+        unit_sb = keep.tile([P, ROW_TILES], F32, name="unit_sb")
+        with nc.allow_non_contiguous_dma(reason="one value a partition and row tile"):
+            nc.sync.dma_start(out=unit_sb[:], in_=unit.rearrange("(t p) o -> p (t o)", p=P))
+        ta_sb = keep.tile([P, U // LIST_ROWS], U16, name="ta_sb")
+        nc.sync.dma_start(ta_sb[:], ta)
+        tb_sb = keep.tile([P, U // LIST_ROWS], U16, name="tb_sb")
+        nc.sync.dma_start(tb_sb[:], tb)
+        om_sb = []
+        for h in range(U // OM_COLS):
+            piece = keep.tile([P, ROW_TILES, OM_COLS], F32, name=f"om{h}")
+            nc.sync.dma_start(
+                out=piece[:], in_=om[:, h * OM_COLS : (h + 1) * OM_COLS].rearrange("(t p) r -> p t r", p=P)
+            )
+            om_sb.append(piece)
+        w3_raw = load_rows("w3", w3)
+
+        w2_q = [[quantize(keep, "w2_0", round_and_interleave("w2_0", w2_raw[0][0], nc.scalar.copy))]]
+        x_codes = []
+        for o in range(PASSES):
+            picked = keep.tile([P, S], U32, name=f"x_codes{o}", align_bytes=64)
+            nc.vector.tensor_copy(picked[:], word_tables[o][:].indirect(offs_sb[:]))
+            x_codes.append(picked)
+        x_scale = keep.tile([P, S], U8, name="x_scale", align_bytes=64)
+        nc.vector.tensor_copy(x_scale[:], scale_table[:].indirect(offs_sb[:]))
+        w2_q.append(
+            [
+                quantize(keep, f"w2_1{h}", round_and_interleave(f"w2_1{h}", w2_raw[1][h], copy))
+                for h, copy in enumerate((nc.scalar.copy, nc.vector.tensor_copy))
+            ]
+        )
+
+        def first_layer(name, pieces, t):
+            acc = bank(name)
+            for o in range(PASSES):
+                width = H // len(pieces[o])
+                codes, scales = pieces[o][t * P // width]
+                cols = slice(t * P % width, t * P % width + P)
+                nc.tensor.matmul_mx(
+                    out=acc[:],
+                    lhsT=codes[:, cols].bitcast(FP8X4),
+                    lhsT_scale=scales[:, cols],
+                    rhs=x_codes[o][:].bitcast(FP8X4),
+                    rhs_scale=x_scale[4 * o : P, :],
+                    start=(o == 0),
+                    stop=(o == PASSES - 1),
+                )
+            return acc
+
+        ys = [first_layer(f"ys{t}", w2_q, t) for t in range(ROW_TILES)]
+        decay = []
+        for t in range(ROW_TILES):
+            size = work.tile([P, S], F32, name="size")
+            nc.scalar.activation(size[:], ys[t][:], ACT.Abs)
+            e = keep.tile([P, S], F32, name=f"decay{t}")
+            nc.scalar.activation(e[:], size[:], ACT.Exp, scale=-1.0)
+            decay.append(e)
+
+        w1_bf = [round_and_interleave(f"w1_{o}", w1_raw[o], nc.vector.tensor_copy) for o in range(PASSES)]
+        w1_q = [[quantize(keep, f"w1_{o}", w1_bf[o])] for o in range(PASSES)]
+        y_acc = [first_layer(f"y{t}", w1_q, t) for t in range(ROW_TILES)]
+
+        root_e = math.exp(0.5)
+        prec, prec_neg, mean = [], [], []
+        for t in range(ROW_TILES):
+            m = keep.tile([P, S], F32, name=f"mean{t}")
+            nc.vector.tensor_scalar(m[:], y_acc[t][:], unit_sb[:, t : t + 1], None, ALU.mult)
+            mean.append(m)
+            tail = work.tile([P, S], F32, name="tail")
+            nc.scalar.activation(tail[:], decay[t][:], ACT.Ln, bias=root_e, scale=root_e)
+            pos = keep.tile([P, S], F32, name=f"prec{t}")
+            nc.vector.scalar_tensor_tensor(pos[:], ys[t][:], 0.0, tail[:], ALU.max, ALU.add)
+            neg = keep.tile([P, S], F32, name=f"prec_neg{t}")
+            nc.vector.tensor_scalar(neg[:], pos[:], -1.0, None, ALU.mult)
+            prec.append(pos)
+            prec_neg.append(neg)
+
+        w3_codes, w3_scales = quantize(keep, "w3", round_and_interleave("w3", w3_raw, nc.vector.tensor_copy))
+
+        def products(c, t):
+            entries = slice(c * CHUNK // LIST_ROWS, (c + 1) * CHUNK // LIST_ROWS)
+            first = c * CHUNK % OM_COLS
+            weight = om_sb[c * CHUNK // OM_COLS][:, t, first : first + CHUNK]
+            prb_neg = work.tile([P, CHUNK], F32, name="prb_neg")
+            nc.scalar.activation(prb_neg[:], prec_neg[t][:].indirect(tb_sb[:, entries]), ACT.Copy)
+            yb = work.tile([P, CHUNK], F32, name="yb")
+            nc.scalar.activation(yb[:], mean[t][:].indirect(tb_sb[:, entries]), ACT.Copy)
+            pa = work.tile([P, CHUNK], F32, name="pa")
+            nc.vector.tensor_tensor(pa[:], prec[t][:].indirect(ta_sb[:, entries]), weight, ALU.mult)
+            pb = work.tile([P, CHUNK], F32, name="pb")
+            nc.vector.scalar_tensor_tensor(pb[:], weight, 1.0, prb_neg[:], ALU.subtract, ALU.mult)
+            na = work.tile([P, CHUNK], F32, name="na")
+            nc.vector.tensor_tensor(na[:], mean[t][:].indirect(ta_sb[:, entries]), pa[:], ALU.mult)
+            nb = work.tile([P, CHUNK], F32, name="nb")
+            nc.vector.tensor_tensor(nb[:], yb[:], pb[:], ALU.mult)
+            return pa, pb, na, nb
+
+        def turn_and_add(acc, t, b, first, second):
+            for n, term in enumerate((first, second)):
+                nc.tensor.matmul(
+                    acc[:, t * P : (t + 1) * P],
+                    lhsT=term[:, b * P : (b + 1) * P],
+                    rhs=ident[:],
+                    start=(n == 0),
+                    stop=(n == 1),
+                    is_transpose=True,
+                )
+
+        def by_word_plane(acc):
+            return acc[:].rearrange("r (p u e) -> r u p e", u=2, e=2)
+
+        def divide(den, num):
+            planes = "r (u p e) -> r u p e"
+            root = work.tile([P, H], F32, name="root")
+            nc.scalar.activation(root[:].rearrange(planes, u=2, e=2), by_word_plane(den), ACT.Abs_reciprocal_sqrt)
+            sign = work.tile([P, H], BF16, name="sign")
+            nc.scalar.activation(sign[:].rearrange(planes, u=2, e=2), by_word_plane(den), ACT.Sign)
+            inverse = work.tile([P, H], F32, name="inverse")
+            nc.scalar.activation(inverse[:], root[:], ACT.Square)
+            unsigned = work.tile([P, H], BF16, name="unsigned")
+            nc.vector.tensor_tensor(
+                unsigned[:].rearrange(planes, u=2, e=2),
+                by_word_plane(num),
+                inverse[:].rearrange(planes, u=2, e=2),
+                ALU.mult,
+            )
+            hid_rows = work.tile([P, H], BF16, name="hid_rows")
+            nc.vector.tensor_tensor(hid_rows[:], unsigned[:], sign[:], ALU.mult)
+            return hid_rows
+
+        def turn_back(hid_blocks):
+            acc = bank("turned")
+            for b, hid_rows in enumerate(hid_blocks):
+                words = hid_rows[:].bitcast(F32)
+                for u in range(2):
+                    at = (2 * b + u) * P
+                    nc.tensor.transpose(acc[:, at : at + P], words[:, u * P : (u + 1) * P], ident[:])
+            grouped = work.tile([P, CHUNK, PACK], BF16, name="hid_grouped", align_bytes=64)
+            nc.scalar.copy(
+                out=grouped[:].rearrange("p r j -> p (r j)").bitcast(F32).rearrange("p (b r u) -> p b r u", b=BLOCKS, u=2),
+                in_=acc[:].rearrange("p (b u r) -> p b r u", b=BLOCKS, u=2),
+            )
+            return grouped
+
+        def last_layer(c, grouped):
+            codes, scales = quantize(work, "hid", grouped)
+            acc = bank("result")
+            nc.tensor.matmul_mx(
+                out=acc[:, 0:CHUNK],
+                lhsT=w3_codes[:].bitcast(FP8X4),
+                lhsT_scale=w3_scales[:],
+                rhs=codes[:].bitcast(FP8X4),
+                rhs_scale=scales[:],
+                start=True,
+                stop=True,
+            )
+            result = work.tile([P, CHUNK], F32, name="result_sb")
+            nc.scalar.copy(result[:], acc[:, 0:CHUNK])
+            nc.sync.dma_start(out=out[:, c * CHUNK : (c + 1) * CHUNK], in_=result[:])
+
+        def finish(c, sums, step, state):
+            if step < BLOCKS:
+                state.append(divide(*sums[step]))
+            elif step == BLOCKS:
+                state.append(turn_back(state[0:BLOCKS]))
+            else:
+                last_layer(c, state[BLOCKS])
+
+        previous = None
+        for c in range(CHUNKS):
+            state = []
+            for t in range(ROW_TILES):
+                pa, pb, na, nb = products(c, t)
+                if previous is not None:
+                    finish(c - 1, previous, t, state)
+                if t == 0:
+                    sums = [(bank("den"), bank("num")) for b in range(BLOCKS)]
+                for b in range(BLOCKS):
+                    turn_and_add(sums[b][0], t, b, pa, pb)
+                    turn_and_add(sums[b][1], t, b, na, nb)
+            previous = sums
+        state = []
+        for step in range(ROW_TILES):
+            finish(CHUNKS - 1, previous, step, state)

@@ -22,11 +22,18 @@ PACK = 4
 K_PASS = P * PACK
 PASSES = K // K_PASS
 ROW_TILES = H // P
-CHUNK = 256
-CHUNKS = U // CHUNK
-BLOCKS = CHUNK // P
+HALF = H // 2
+BLOCKS = U // P
 LIST_ROWS = 16
-OM_COLS = 512
+WINDOW = S + LIST_ROWS
+WIDE = 512
+LAST_WIDTHS = [256,128,128]
+EARLY = 0
+THREE = []
+BFUSED = [9]
+VSQ = []
+CAST_ON_SCALAR = ["w2_00","w2_10","w2_01"]
+CLAMP = 30.0
 
 
 def tile_picked_ycovin_mean_p_kernel(
@@ -43,7 +50,24 @@ def tile_picked_ycovin_mean_p_kernel(
             nc.sync.dma_start(out=raw[:], in_=rows.rearrange("(p j) c -> p j c", j=PACK))
             return raw
 
-        def round_and_interleave(name, raw, copy):
+        def load_list(name, source):
+            tile = keep.tile(list(source.shape), U16, name=name)
+            nc.sync.dma_start(tile[:], source)
+            return tile
+
+        def load_half(name, w, h):
+            return [
+                load_rows(f"{name}_{o}{h}", w[o * K_PASS : (o + 1) * K_PASS, h * HALF : (h + 1) * HALF])
+                for o in range(PASSES)
+            ]
+
+        def load_om(t):
+            tile = keep.tile([P, U], F32, name=f"om{t}")
+            nc.sync.dma_start(out=tile[:], in_=om[t * P : (t + 1) * P, :])
+            return tile
+
+        def round_and_interleave(name, raw):
+            copy = nc.scalar.copy if name in CAST_ON_SCALAR else nc.vector.tensor_copy
             grouped = keep.tile([P, raw.shape[2], PACK], BF16, name=name + "_bf16", align_bytes=64)
             copy(
                 out=grouped[:].rearrange("p (c i) j -> p c j i", i=4),
@@ -63,44 +87,56 @@ def tile_picked_ycovin_mean_p_kernel(
         def bank(name):
             return psum.tile([P, 512], F32, name=name, tag="bank")
 
+        def window(name):
+            tile = keep.tile([P, WINDOW], F32, name=name)
+            nc.gpsimd.memset(tile[:, S:WINDOW], 0.0)
+            return tile
+
         scale_table = keep.tile([P, T], U8, name="scale_table", align_bytes=64)
-        nc.gpsimd.memset(scale_table[:], 0)
+        nc.gpsimd.memset(scale_table[:].bitcast(I32), 0)
         ident = keep.tile([P, P], F32, name="ident")
         make_identity(nc, ident[:])
+        prec = [window(f"prec{t}") for t in range(ROW_TILES)]
+        mean = [window(f"mean{t}") for t in range(ROW_TILES)]
 
-        half = H // 2
-        w2_raw = [[load_rows("w2_0", w2[0:K_PASS, :])]]
-        offs_sb = keep.tile([P, S // LIST_ROWS], U16, name="offs_sb")
-        nc.sync.dma_start(offs_sb[:], offs)
-        word_tables = []
-        for o in range(PASSES):
+        word_tables, om_sb = [], []
+        w2_raw, w1_raw = [[], []], [[], []]
+
+        def load_words(o):
             table = keep.tile([P, T], U32, name=f"word_table{o}", align_bytes=64)
             nc.sync.dma_start(out=table[:].bitcast(I32), in_=x_words[o].rearrange("p n t -> p (n t)").bitcast(I32))
             word_tables.append(table)
+
+        def load_piece(name, w, raw, o, h):
+            raw[h].append(load_rows(f"{name}_{o}{h}", w[o * K_PASS : (o + 1) * K_PASS, h * HALF : (h + 1) * HALF]))
+
+        offs_sb = load_list("offs_sb", offs)
+        load_words(0)
+        load_words(1)
         for q in range(4):
             nc.sync.dma_start(
                 out=scale_table[32 * q : 32 * q + 4 * PASSES, :].bitcast(I32),
                 in_=x_scales.bitcast(I32)[:, 4 * q : 4 * q + 4, :],
             )
-        w2_raw.append([load_rows(f"w2_1{h}", w2[K_PASS:K, h * half : (h + 1) * half]) for h in range(2)])
-        w1_raw = [load_rows(f"w1_{o}", w1[o * K_PASS : (o + 1) * K_PASS, :]) for o in range(PASSES)]
+        load_piece("w2", w2, w2_raw, 0, 0)
+        load_piece("w2", w2, w2_raw, 1, 0)
+        load_piece("w2", w2, w2_raw, 0, 1)
+        load_piece("w2", w2, w2_raw, 1, 1)
         unit_sb = keep.tile([P, ROW_TILES], F32, name="unit_sb")
         with nc.allow_non_contiguous_dma(reason="one value a partition and row tile"):
             nc.sync.dma_start(out=unit_sb[:], in_=unit.rearrange("(t p) o -> p (t o)", p=P))
-        ta_sb = keep.tile([P, U // LIST_ROWS], U16, name="ta_sb")
-        nc.sync.dma_start(ta_sb[:], ta)
-        tb_sb = keep.tile([P, U // LIST_ROWS], U16, name="tb_sb")
-        nc.sync.dma_start(tb_sb[:], tb)
-        om_sb = []
-        for h in range(U // OM_COLS):
-            piece = keep.tile([P, ROW_TILES, OM_COLS], F32, name=f"om{h}")
-            nc.sync.dma_start(
-                out=piece[:], in_=om[:, h * OM_COLS : (h + 1) * OM_COLS].rearrange("(t p) r -> p t r", p=P)
-            )
-            om_sb.append(piece)
+        ta_sb = load_list("ta_sb", ta)
+        tb_sb = load_list("tb_sb", tb)
+        load_piece("w1", w1, w1_raw, 0, 0)
+        load_piece("w1", w1, w1_raw, 1, 0)
+        om_sb.append(load_om(0))
+        load_piece("w1", w1, w1_raw, 0, 1)
+        load_piece("w1", w1, w1_raw, 1, 1)
+        om_sb.append(load_om(1))
+        om_sb.append(load_om(2))
+        om_sb.append(load_om(3))
         w3_raw = load_rows("w3", w3)
 
-        w2_q = [[quantize(keep, "w2_0", round_and_interleave("w2_0", w2_raw[0][0], nc.scalar.copy))]]
         x_codes = []
         for o in range(PASSES):
             picked = keep.tile([P, S], U32, name=f"x_codes{o}", align_bytes=64)
@@ -108,130 +144,138 @@ def tile_picked_ycovin_mean_p_kernel(
             x_codes.append(picked)
         x_scale = keep.tile([P, S], U8, name="x_scale", align_bytes=64)
         nc.vector.tensor_copy(x_scale[:], scale_table[:].indirect(offs_sb[:]))
-        w2_q.append(
-            [
-                quantize(keep, f"w2_1{h}", round_and_interleave(f"w2_1{h}", w2_raw[1][h], copy))
-                for h, copy in enumerate((nc.scalar.copy, nc.vector.tensor_copy))
-            ]
-        )
 
-        def first_layer(name, pieces, t):
-            acc = bank(name)
-            for o in range(PASSES):
-                width = H // len(pieces[o])
-                codes, scales = pieces[o][t * P // width]
-                cols = slice(t * P % width, t * P % width + P)
-                nc.tensor.matmul_mx(
-                    out=acc[:],
-                    lhsT=codes[:, cols].bitcast(FP8X4),
-                    lhsT_scale=scales[:, cols],
-                    rhs=x_codes[o][:].bitcast(FP8X4),
-                    rhs_scale=x_scale[4 * o : P, :],
-                    start=(o == 0),
-                    stop=(o == PASSES - 1),
-                )
-            return acc
+        def first_layer(name, raw, h):
+            rounded = [round_and_interleave(f"{name}_{o}{h}", raw[h][o]) for o in range(PASSES)]
+            packed = [quantize(keep, f"{name}_{o}{h}", rounded[o]) for o in range(PASSES)]
+            sums = []
+            for first in range(0, HALF, P):
+                acc = bank(f"{name}_acc")
+                for o in range(PASSES):
+                    codes, scales = packed[o]
+                    nc.tensor.matmul_mx(
+                        out=acc[:],
+                        lhsT=codes[:, first : first + P].bitcast(FP8X4),
+                        lhsT_scale=scales[:, first : first + P],
+                        rhs=x_codes[o][:].bitcast(FP8X4),
+                        rhs_scale=x_scale[4 * o : P, :],
+                        start=(o == 0),
+                        stop=(o == PASSES - 1),
+                    )
+                sums.append(acc)
+            return sums
 
-        ys = [first_layer(f"ys{t}", w2_q, t) for t in range(ROW_TILES)]
-        decay = []
+        ys = first_layer("w2", w2_raw, 0) + first_layer("w2", w2_raw, 1)
+        bounded = keep.tile([P, ROW_TILES, S], F32, name="bounded")
+        growth = keep.tile([P, ROW_TILES, S], F32, name="growth")
         for t in range(ROW_TILES):
-            size = work.tile([P, S], F32, name="size")
-            nc.scalar.activation(size[:], ys[t][:], ACT.Abs)
-            e = keep.tile([P, S], F32, name=f"decay{t}")
-            nc.scalar.activation(e[:], size[:], ACT.Exp, scale=-1.0)
-            decay.append(e)
+            nc.vector.tensor_scalar(bounded[:, t, :], ys[t][:], CLAMP, None, ALU.min)
+            if t % 2 == 1:
+                nc.scalar.activation(growth[:, t - 1 : t + 1, :], bounded[:, t - 1 : t + 1, :], ACT.Exp)
 
-        w1_bf = [round_and_interleave(f"w1_{o}", w1_raw[o], nc.vector.tensor_copy) for o in range(PASSES)]
-        w1_q = [[quantize(keep, f"w1_{o}", w1_bf[o])] for o in range(PASSES)]
-        y_acc = [first_layer(f"y{t}", w1_q, t) for t in range(ROW_TILES)]
+        def means(h):
+            for t, acc in enumerate(first_layer("w1", w1_raw, h), start=2 * h):
+                nc.scalar.activation(mean[t][:, 0:S], acc[:], ACT.Copy, scale=unit_sb[:, t : t + 1])
 
+        means(0)
         root_e = math.exp(0.5)
-        prec, prec_neg, mean = [], [], []
         for t in range(ROW_TILES):
-            m = keep.tile([P, S], F32, name=f"mean{t}")
-            nc.vector.tensor_scalar(m[:], y_acc[t][:], unit_sb[:, t : t + 1], None, ALU.mult)
-            mean.append(m)
-            tail = work.tile([P, S], F32, name="tail")
-            nc.scalar.activation(tail[:], decay[t][:], ACT.Ln, bias=root_e, scale=root_e)
-            pos = keep.tile([P, S], F32, name=f"prec{t}")
-            nc.vector.scalar_tensor_tensor(pos[:], ys[t][:], 0.0, tail[:], ALU.max, ALU.add)
-            neg = keep.tile([P, S], F32, name=f"prec_neg{t}")
-            nc.vector.tensor_scalar(neg[:], pos[:], -1.0, None, ALU.mult)
-            prec.append(pos)
-            prec_neg.append(neg)
+            log = bounded[:, (t + 2) % ROW_TILES, :]
+            nc.scalar.activation(log, growth[:, t, :], ACT.Ln, bias=root_e, scale=root_e)
+            nc.vector.scalar_tensor_tensor(prec[t][:, 0:S], ys[t][:], 0.5, log, ALU.add, ALU.max)
 
-        w3_codes, w3_scales = quantize(keep, "w3", round_and_interleave("w3", w3_raw, nc.vector.tensor_copy))
-
-        def products(c, t):
-            entries = slice(c * CHUNK // LIST_ROWS, (c + 1) * CHUNK // LIST_ROWS)
-            first = c * CHUNK % OM_COLS
-            weight = om_sb[c * CHUNK // OM_COLS][:, t, first : first + CHUNK]
-            prb_neg = work.tile([P, CHUNK], F32, name="prb_neg")
-            nc.scalar.activation(prb_neg[:], prec_neg[t][:].indirect(tb_sb[:, entries]), ACT.Copy)
-            yb = work.tile([P, CHUNK], F32, name="yb")
-            nc.scalar.activation(yb[:], mean[t][:].indirect(tb_sb[:, entries]), ACT.Copy)
-            pa = work.tile([P, CHUNK], F32, name="pa")
-            nc.vector.tensor_tensor(pa[:], prec[t][:].indirect(ta_sb[:, entries]), weight, ALU.mult)
-            pb = work.tile([P, CHUNK], F32, name="pb")
+        def products(n, t, first, width):
+            entries = slice(first // LIST_ROWS, (first + width) // LIST_ROWS)
+            weight = om_sb[t][:, first : first + width]
+            prb_neg = work.tile([P, width], F32, name="prb_neg")
+            nc.scalar.activation(prb_neg[:], prec[t][:].indirect(tb_sb[:, entries]), ACT.Copy, scale=-1.0)
+            yb = work.tile([P, width], F32, name="yb", bufs=4)
+            if n < EARLY:
+                nc.vector.tensor_copy(yb[:], mean[t][:].indirect(tb_sb[:, entries]))
+            elif n not in BFUSED:
+                nc.scalar.activation(yb[:], mean[t][:].indirect(tb_sb[:, entries]), ACT.Copy)
+            pa = work.tile([P, width], F32, name="pa")
+            if n in THREE:
+                pra = work.tile([P, width], F32, name="pra")
+                nc.scalar.activation(pra[:], prec[t][:].indirect(ta_sb[:, entries]), ACT.Copy)
+                nc.vector.tensor_tensor(pa[:], pra[:], weight, ALU.mult)
+            else:
+                nc.vector.tensor_tensor(pa[:], prec[t][:].indirect(ta_sb[:, entries]), weight, ALU.mult)
+            pb = work.tile([P, width], F32, name="pb")
             nc.vector.scalar_tensor_tensor(pb[:], weight, 1.0, prb_neg[:], ALU.subtract, ALU.mult)
-            na = work.tile([P, CHUNK], F32, name="na")
+            na = work.tile([P, width], F32, name="na")
             nc.vector.tensor_tensor(na[:], mean[t][:].indirect(ta_sb[:, entries]), pa[:], ALU.mult)
-            nb = work.tile([P, CHUNK], F32, name="nb")
-            nc.vector.tensor_tensor(nb[:], yb[:], pb[:], ALU.mult)
+            nb = work.tile([P, width], F32, name="nb")
+            if n in BFUSED:
+                nc.vector.tensor_tensor(nb[:], mean[t][:].indirect(tb_sb[:, entries]), pb[:], ALU.mult)
+            else:
+                nc.vector.tensor_tensor(nb[:], yb[:], pb[:], ALU.mult)
             return pa, pb, na, nb
 
-        def turn_and_add(acc, t, b, first, second):
-            for n, term in enumerate((first, second)):
-                nc.tensor.matmul(
-                    acc[:, t * P : (t + 1) * P],
-                    lhsT=term[:, b * P : (b + 1) * P],
-                    rhs=ident[:],
-                    start=(n == 0),
-                    stop=(n == 1),
-                    is_transpose=True,
+        def turn_and_add(name, width, left, right):
+            acc = bank(name)
+            for at in range(0, width, P):
+                for n, term in enumerate((left, right)):
+                    nc.tensor.matmul(
+                        acc[:, at : at + P],
+                        lhsT=term[:, at : at + P],
+                        rhs=ident[:],
+                        start=(n == 0),
+                        stop=(n == 1),
+                        is_transpose=True,
+                    )
+            return acc[:, 0:width].rearrange("r (q u e) -> r u q e", u=2, e=2)
+
+        hid_rows = keep.tile([P, BLOCKS, 2, HALF], BF16, name="hid_rows")
+
+        def divide(n, t, first, width, den, num):
+            planes = "r (u q e) -> r u q e"
+            root = work.tile([P, width], F32, name="root")
+            nc.scalar.activation(root[:].rearrange(planes, u=2, e=2), den, ACT.Abs_reciprocal_sqrt)
+            sign = work.tile([P, width], BF16, name="sign")
+            inverse = work.tile([P, width], F32, name="inverse")
+            unsigned = work.tile([P, width], BF16, name="unsigned")
+            if n in VSQ:
+                nc.scalar.activation(sign[:].rearrange(planes, u=2, e=2), den, ACT.Sign)
+                nc.vector.tensor_tensor(
+                    inverse[:].rearrange(planes, u=2, e=2), num, root[:].rearrange(planes, u=2, e=2), ALU.mult
                 )
-
-        def by_word_plane(acc):
-            return acc[:].rearrange("r (p u e) -> r u p e", u=2, e=2)
-
-        def divide(den, num):
-            planes = "r (u p e) -> r u p e"
-            root = work.tile([P, H], F32, name="root")
-            nc.scalar.activation(root[:].rearrange(planes, u=2, e=2), by_word_plane(den), ACT.Abs_reciprocal_sqrt)
-            sign = work.tile([P, H], BF16, name="sign")
-            nc.scalar.activation(sign[:].rearrange(planes, u=2, e=2), by_word_plane(den), ACT.Sign)
-            inverse = work.tile([P, H], F32, name="inverse")
-            nc.scalar.activation(inverse[:], root[:], ACT.Square)
-            unsigned = work.tile([P, H], BF16, name="unsigned")
+                nc.vector.tensor_tensor(unsigned[:], inverse[:], root[:], ALU.mult)
+            else:
+                nc.scalar.activation(sign[:].rearrange(planes, u=2, e=2), den, ACT.Sign)
+                nc.scalar.activation(inverse[:], root[:], ACT.Square)
+                nc.vector.tensor_tensor(
+                    unsigned[:].rearrange(planes, u=2, e=2), num, inverse[:].rearrange(planes, u=2, e=2), ALU.mult
+                )
+            run = P // 2
+            target = hid_rows[:, first // P : (first + width) // P, :, t * run : (t + 1) * run]
             nc.vector.tensor_tensor(
-                unsigned[:].rearrange(planes, u=2, e=2),
-                by_word_plane(num),
-                inverse[:].rearrange(planes, u=2, e=2),
+                target.rearrange("r b u c -> r u b c"),
+                unsigned[:].rearrange("r (u b c) -> r u b c", u=2, c=run),
+                sign[:].rearrange("r (u b c) -> r u b c", u=2, c=run),
                 ALU.mult,
             )
-            hid_rows = work.tile([P, H], BF16, name="hid_rows")
-            nc.vector.tensor_tensor(hid_rows[:], unsigned[:], sign[:], ALU.mult)
-            return hid_rows
 
-        def turn_back(hid_blocks):
+        def turn_back(first, width):
+            blocks = width // P
             acc = bank("turned")
-            for b, hid_rows in enumerate(hid_blocks):
-                words = hid_rows[:].bitcast(F32)
+            for b in range(blocks):
                 for u in range(2):
                     at = (2 * b + u) * P
-                    nc.tensor.transpose(acc[:, at : at + P], words[:, u * P : (u + 1) * P], ident[:])
-            grouped = work.tile([P, CHUNK, PACK], BF16, name="hid_grouped", align_bytes=64)
+                    words = hid_rows[:, first // P + b, u, :].bitcast(F32)
+                    nc.tensor.transpose(acc[:, at : at + P], words, ident[:])
+            grouped = work.tile([P, width, PACK], BF16, name="hid_grouped", align_bytes=64)
             nc.scalar.copy(
-                out=grouped[:].rearrange("p r j -> p (r j)").bitcast(F32).rearrange("p (b r u) -> p b r u", b=BLOCKS, u=2),
-                in_=acc[:].rearrange("p (b u r) -> p b r u", b=BLOCKS, u=2),
+                out=grouped[:].rearrange("p r j -> p (r j)").bitcast(F32).rearrange("p (b r u) -> p b r u", b=blocks, u=2),
+                in_=acc[:, 0 : 2 * width].rearrange("p (b u r) -> p b r u", b=blocks, u=2),
             )
             return grouped
 
-        def last_layer(c, grouped):
+        def last_layer(first, width, grouped, copy):
             codes, scales = quantize(work, "hid", grouped)
             acc = bank("result")
             nc.tensor.matmul_mx(
-                out=acc[:, 0:CHUNK],
+                out=acc[:, 0:width],
                 lhsT=w3_codes[:].bitcast(FP8X4),
                 lhsT_scale=w3_scales[:],
                 rhs=codes[:].bitcast(FP8X4),
@@ -239,31 +283,31 @@ def tile_picked_ycovin_mean_p_kernel(
                 start=True,
                 stop=True,
             )
-            result = work.tile([P, CHUNK], F32, name="result_sb")
-            nc.scalar.copy(result[:], acc[:, 0:CHUNK])
-            nc.sync.dma_start(out=out[:, c * CHUNK : (c + 1) * CHUNK], in_=result[:])
+            result = work.tile([P, width], F32, name="result_sb")
+            copy(result[:], acc[:, 0:width])
+            nc.sync.dma_start(out=out[:, first : first + width], in_=result[:])
 
-        def finish(c, sums, step, state):
-            if step < BLOCKS:
-                state.append(divide(*sums[step]))
-            elif step == BLOCKS:
-                state.append(turn_back(state[0:BLOCKS]))
-            else:
-                last_layer(c, state[BLOCKS])
-
-        previous = None
-        for c in range(CHUNKS):
-            state = []
-            for t in range(ROW_TILES):
-                pa, pb, na, nb = products(c, t)
-                if previous is not None:
-                    finish(c - 1, previous, t, state)
-                if t == 0:
-                    sums = [(bank("den"), bank("num")) for b in range(BLOCKS)]
-                for b in range(BLOCKS):
-                    turn_and_add(sums[b][0], t, b, pa, pb)
-                    turn_and_add(sums[b][1], t, b, na, nb)
-            previous = sums
-        state = []
-        for step in range(ROW_TILES):
-            finish(CHUNKS - 1, previous, step, state)
+        last = ROW_TILES - 1
+        steps = [(t, 0, WIDE) for t in range(ROW_TILES)] + [(t, WIDE, WIDE) for t in range(last)]
+        steps.extend((last, WIDE + sum(LAST_WIDTHS[0:n]), width) for n, width in enumerate(LAST_WIDTHS))
+        sums, whole, turned = {}, [], []
+        for n in range(len(steps) + 3):
+            if n == 1:
+                means(1)
+            if n == 2:
+                w3_codes, w3_scales = quantize(keep, "w3", round_and_interleave("w3", w3_raw))
+            if n < len(steps):
+                pa, pb, na, nb = products(n, *steps[n])
+            if turned:
+                last_layer(*turned.pop(0), nc.vector.tensor_copy if n in [] else nc.scalar.copy)
+            if whole:
+                first, width = whole.pop(0)
+                turned.append((first, width, turn_back(first, width)))
+            if 0 <= n - 1 < len(steps):
+                t, first, width = steps[n - 1]
+                divide(n - 1, t, first, width, *sums[n - 1])
+                if t == last:
+                    whole.extend((at, min(width, HALF)) for at in range(first, first + width, HALF))
+            if n < len(steps):
+                width = steps[n][2]
+                sums[n] = (turn_and_add("den", width, pa, pb), turn_and_add("num", width, na, nb))

@@ -21,19 +21,19 @@ P = 128
 PACK = 4
 K_PASS = P * PACK
 PASSES = K // K_PASS
+QUADRANT = 32
+SCALE_ROWS = 4
 ROW_TILES = H // P
 HALF = H // 2
-BLOCKS = U // P
+BANK = 512
+BANKS = 8
 LIST_ROWS = 16
 WINDOW = S + LIST_ROWS
-WIDE = 512
-LAST_WIDTHS = [256,128,128]
-EARLY = 0
-THREE = []
-BFUSED = [9]
-VSQ = []
-CAST_ON_SCALAR = ["w2_00","w2_10","w2_01"]
-CLAMP = 30.0
+WIDE = BANK
+TURN = BANK // 2
+LAST_WIDTHS = [256, 128, 128]
+WORK_BUFS = 3
+TINY = 1e-15
 
 
 def tile_picked_ycovin_mean_p_kernel(
@@ -42,50 +42,29 @@ def tile_picked_ycovin_mean_p_kernel(
     nc = tc.nc
     with ExitStack() as ctx:
         keep = ctx.enter_context(tc.tile_pool(name="keep", bufs=1))
-        work = ctx.enter_context(tc.tile_pool(name="work", bufs=3))
-        psum = ctx.enter_context(tc.psum_pool(name="psum", bufs=8))
+        work = ctx.enter_context(tc.tile_pool(name="work", bufs=WORK_BUFS))
+        psum = ctx.enter_context(tc.psum_pool(name="psum", bufs=BANKS))
 
-        def load_rows(name, rows):
-            raw = keep.tile([P, PACK, rows.shape[1]], F32, name=name + "_raw")
-            nc.sync.dma_start(out=raw[:], in_=rows.rearrange("(p j) c -> p j c", j=PACK))
-            return raw
+        def bank(name):
+            return psum.tile([P, BANK], F32, name=name, tag="bank")
 
         def load_list(name, source):
             tile = keep.tile(list(source.shape), U16, name=name)
             nc.sync.dma_start(tile[:], source)
             return tile
 
-        def load_half(name, w, h):
-            return [
-                load_rows(f"{name}_{o}{h}", w[o * K_PASS : (o + 1) * K_PASS, h * HALF : (h + 1) * HALF])
-                for o in range(PASSES)
-            ]
-
-        def load_om(t):
-            tile = keep.tile([P, U], F32, name=f"om{t}")
-            nc.sync.dma_start(out=tile[:], in_=om[t * P : (t + 1) * P, :])
+        def load_words(o):
+            tile = keep.tile([P, T], U32, name=f"word_table{o}", align_bytes=64)
+            nc.sync.dma_start(out=tile[:].bitcast(I32), in_=x_words[o].rearrange("p n j -> p (n j)").bitcast(I32))
             return tile
 
-        def round_and_interleave(name, raw):
-            copy = nc.scalar.copy if name in CAST_ON_SCALAR else nc.vector.tensor_copy
-            grouped = keep.tile([P, raw.shape[2], PACK], BF16, name=name + "_bf16", align_bytes=64)
-            copy(
-                out=grouped[:].rearrange("p (c i) j -> p c j i", i=4),
-                in_=raw[:].rearrange("p j (c i) -> p c j i", i=4),
-            )
-            return grouped
+        def load_rows(name, rows):
+            tile = keep.tile([P, PACK, rows.shape[1]], F32, name=name + "_raw")
+            nc.sync.dma_start(out=tile[:], in_=rows.rearrange("(p j) c -> p j c", j=PACK))
+            return tile
 
-        def quantize(pool, name, grouped):
-            width = grouped.shape[1]
-            codes = pool.tile([P, width], U32, name=name + "_codes", align_bytes=64)
-            scales = pool.tile([P, width], U8, name=name + "_scales", align_bytes=64)
-            nc.vector.quantize_mx(
-                out=codes[:].bitcast(FP8X4), scales=scales[:], in_=grouped[:].rearrange("p c j -> p (c j)")
-            )
-            return codes, scales
-
-        def bank(name):
-            return psum.tile([P, 512], F32, name=name, tag="bank")
+        def load_piece(name, w, o, h):
+            return load_rows(f"{name}_{o}{h}", w[o * K_PASS : (o + 1) * K_PASS, h * HALF : (h + 1) * HALF])
 
         def window(name):
             tile = keep.tile([P, WINDOW], F32, name=name)
@@ -96,120 +75,112 @@ def tile_picked_ycovin_mean_p_kernel(
         nc.gpsimd.memset(scale_table[:].bitcast(I32), 0)
         ident = keep.tile([P, P], F32, name="ident")
         make_identity(nc, ident[:])
-        prec = [window(f"prec{t}") for t in range(ROW_TILES)]
+        prec_neg = [window(f"prec_neg{t}") for t in range(ROW_TILES)]
         mean = [window(f"mean{t}") for t in range(ROW_TILES)]
 
-        word_tables, om_sb = [], []
-        w2_raw, w1_raw = [[], []], [[], []]
-
-        def load_words(o):
-            table = keep.tile([P, T], U32, name=f"word_table{o}", align_bytes=64)
-            nc.sync.dma_start(out=table[:].bitcast(I32), in_=x_words[o].rearrange("p n t -> p (n t)").bitcast(I32))
-            word_tables.append(table)
-
-        def load_piece(name, w, raw, o, h):
-            raw[h].append(load_rows(f"{name}_{o}{h}", w[o * K_PASS : (o + 1) * K_PASS, h * HALF : (h + 1) * HALF]))
-
         offs_sb = load_list("offs_sb", offs)
-        load_words(0)
-        load_words(1)
-        for q in range(4):
+        word_tables = [load_words(0)]
+        for q in range(P // QUADRANT):
             nc.sync.dma_start(
-                out=scale_table[32 * q : 32 * q + 4 * PASSES, :].bitcast(I32),
-                in_=x_scales.bitcast(I32)[:, 4 * q : 4 * q + 4, :],
+                out=scale_table[QUADRANT * q : QUADRANT * q + SCALE_ROWS * PASSES, :].bitcast(I32),
+                in_=x_scales.bitcast(I32)[:, SCALE_ROWS * q : SCALE_ROWS * (q + 1), :],
             )
-        load_piece("w2", w2, w2_raw, 0, 0)
-        load_piece("w2", w2, w2_raw, 1, 0)
-        load_piece("w2", w2, w2_raw, 0, 1)
-        load_piece("w2", w2, w2_raw, 1, 1)
+        w2_raw = {(0, 0): load_piece("w2", w2, 0, 0)}
+        word_tables.append(load_words(1))
+        for o, h in ((1, 0), (0, 1), (1, 1)):
+            w2_raw[o, h] = load_piece("w2", w2, o, h)
+        w1_raw = {(o, 0): load_piece("w1", w1, o, 0) for o in range(PASSES)}
         unit_sb = keep.tile([P, ROW_TILES], F32, name="unit_sb")
         with nc.allow_non_contiguous_dma(reason="one value a partition and row tile"):
-            nc.sync.dma_start(out=unit_sb[:], in_=unit.rearrange("(t p) o -> p (t o)", p=P))
+            nc.sync.dma_start(out=unit_sb[:], in_=unit.rearrange("(t p) one -> p (t one)", p=P))
         ta_sb = load_list("ta_sb", ta)
         tb_sb = load_list("tb_sb", tb)
-        load_piece("w1", w1, w1_raw, 0, 0)
-        load_piece("w1", w1, w1_raw, 1, 0)
-        om_sb.append(load_om(0))
-        load_piece("w1", w1, w1_raw, 0, 1)
-        load_piece("w1", w1, w1_raw, 1, 1)
-        om_sb.append(load_om(1))
-        om_sb.append(load_om(2))
-        om_sb.append(load_om(3))
+        for o in range(PASSES):
+            w1_raw[o, 1] = load_piece("w1", w1, o, 1)
+        om_sb = []
+        for t in range(ROW_TILES):
+            om_sb.append(keep.tile([P, U], F32, name=f"om{t}"))
+            nc.sync.dma_start(out=om_sb[t][:], in_=om[t * P : (t + 1) * P, :])
         w3_raw = load_rows("w3", w3)
 
         x_codes = []
         for o in range(PASSES):
-            picked = keep.tile([P, S], U32, name=f"x_codes{o}", align_bytes=64)
-            nc.vector.tensor_copy(picked[:], word_tables[o][:].indirect(offs_sb[:]))
-            x_codes.append(picked)
+            x_codes.append(keep.tile([P, S], U32, name=f"x_codes{o}", align_bytes=64))
+            nc.vector.tensor_copy(x_codes[o][:], word_tables[o][:].indirect(offs_sb[:]))
         x_scale = keep.tile([P, S], U8, name="x_scale", align_bytes=64)
         nc.vector.tensor_copy(x_scale[:], scale_table[:].indirect(offs_sb[:]))
 
-        def first_layer(name, raw, h):
-            rounded = [round_and_interleave(f"{name}_{o}{h}", raw[h][o]) for o in range(PASSES)]
+        def round_and_interleave(name, raw, factor, on_scalar):
+            tile = keep.tile([P, raw.shape[2], PACK], BF16, name=name + "_bf16", align_bytes=64)
+            target = tile[:].rearrange("p (c i) j -> p c j i", i=4)
+            source = raw[:].rearrange("p j (c i) -> p c j i", i=4)
+            if on_scalar:
+                nc.scalar.activation(target, source, ACT.Copy, scale=factor)
+            else:
+                nc.vector.tensor_scalar(target, source, factor, None, ALU.mult)
+            return tile
+
+        def quantize(pool, name, interleaved):
+            columns = interleaved.shape[1]
+            codes = pool.tile([P, columns], U32, name=name + "_codes", align_bytes=64)
+            scales = pool.tile([P, columns], U8, name=name + "_scales", align_bytes=64)
+            nc.vector.quantize_mx(
+                out=codes[:].bitcast(FP8X4), scales=scales[:], in_=interleaved[:].rearrange("p c j -> p (c j)")
+            )
+            return codes, scales
+
+        def first_layer(name, raw, h, factor, on_scalar):
+            rounded = [round_and_interleave(f"{name}_{o}{h}", raw[o, h], factor, on_scalar) for o in range(PASSES)]
             packed = [quantize(keep, f"{name}_{o}{h}", rounded[o]) for o in range(PASSES)]
-            sums = []
-            for first in range(0, HALF, P):
+            banks = []
+            for column in range(0, HALF, P):
                 acc = bank(f"{name}_acc")
-                for o in range(PASSES):
-                    codes, scales = packed[o]
+                for o, (codes, scales) in enumerate(packed):
                     nc.tensor.matmul_mx(
                         out=acc[:],
-                        lhsT=codes[:, first : first + P].bitcast(FP8X4),
-                        lhsT_scale=scales[:, first : first + P],
+                        lhsT=codes[:, column : column + P].bitcast(FP8X4),
+                        lhsT_scale=scales[:, column : column + P],
                         rhs=x_codes[o][:].bitcast(FP8X4),
-                        rhs_scale=x_scale[4 * o : P, :],
+                        rhs_scale=x_scale[SCALE_ROWS * o : P, :],
                         start=(o == 0),
                         stop=(o == PASSES - 1),
                     )
-                sums.append(acc)
-            return sums
+                banks.append(acc)
+            return banks
 
-        ys = first_layer("w2", w2_raw, 0) + first_layer("w2", w2_raw, 1)
-        bounded = keep.tile([P, ROW_TILES, S], F32, name="bounded")
-        growth = keep.tile([P, ROW_TILES, S], F32, name="growth")
+        z = first_layer("w2", w2_raw, 0, -1.0, True) + first_layer("w2", w2_raw, 1, -1.0, False)
+
+        slot = [0, 2, 3, 1]
+        sigmoid = keep.tile([P, ROW_TILES, S], F32, name="sigmoid")
         for t in range(ROW_TILES):
-            nc.vector.tensor_scalar(bounded[:, t, :], ys[t][:], CLAMP, None, ALU.min)
-            if t % 2 == 1:
-                nc.scalar.activation(growth[:, t - 1 : t + 1, :], bounded[:, t - 1 : t + 1, :], ACT.Exp)
+            nc.scalar.activation(sigmoid[:, slot[t], :], z[t][:], ACT.Sigmoid)
+        outer_logs = keep.tile([P, 2, S], F32, name="outer_logs")
+        nc.scalar.activation(outer_logs[:], sigmoid[:, 0:2, :], ACT.Ln, bias=TINY, scale=math.exp(-0.5))
+        inner_logs = sigmoid[:, 0:2, :]
+        nc.scalar.activation(inner_logs, sigmoid[:, 2:4, :], ACT.Ln, bias=TINY, scale=math.exp(-0.5))
+        logs = [outer_logs[:, 0, :], inner_logs[:, 0, :], inner_logs[:, 1, :], outer_logs[:, 1, :]]
+        for t in range(ROW_TILES):
+            nc.vector.scalar_tensor_tensor(prec_neg[t][:, 0:S], z[t][:], -0.5, logs[t], ALU.add, ALU.min)
 
         def means(h):
-            for t, acc in enumerate(first_layer("w1", w1_raw, h), start=2 * h):
+            for t, acc in enumerate(first_layer("w1", w1_raw, h, 1.0, False), start=2 * h):
                 nc.scalar.activation(mean[t][:, 0:S], acc[:], ACT.Copy, scale=unit_sb[:, t : t + 1])
 
-        means(0)
-        root_e = math.exp(0.5)
-        for t in range(ROW_TILES):
-            log = bounded[:, (t + 2) % ROW_TILES, :]
-            nc.scalar.activation(log, growth[:, t, :], ACT.Ln, bias=root_e, scale=root_e)
-            nc.vector.scalar_tensor_tensor(prec[t][:, 0:S], ys[t][:], 0.5, log, ALU.add, ALU.max)
-
-        def products(n, t, first, width):
+        def products(t, first, width):
             entries = slice(first // LIST_ROWS, (first + width) // LIST_ROWS)
             weight = om_sb[t][:, first : first + width]
-            prb_neg = work.tile([P, width], F32, name="prb_neg")
-            nc.scalar.activation(prb_neg[:], prec[t][:].indirect(tb_sb[:, entries]), ACT.Copy, scale=-1.0)
-            yb = work.tile([P, width], F32, name="yb", bufs=4)
-            if n < EARLY:
-                nc.vector.tensor_copy(yb[:], mean[t][:].indirect(tb_sb[:, entries]))
-            elif n not in BFUSED:
-                nc.scalar.activation(yb[:], mean[t][:].indirect(tb_sb[:, entries]), ACT.Copy)
+            prb = work.tile([P, width], F32, name="prb")
+            nc.scalar.activation(prb[:], prec_neg[t][:].indirect(tb_sb[:, entries]), ACT.Copy, scale=-1.0)
+            yb = work.tile([P, width], F32, name="yb", bufs=WORK_BUFS + 1)
+            nc.scalar.activation(yb[:], mean[t][:].indirect(tb_sb[:, entries]), ACT.Copy)
             pa = work.tile([P, width], F32, name="pa")
-            if n in THREE:
-                pra = work.tile([P, width], F32, name="pra")
-                nc.scalar.activation(pra[:], prec[t][:].indirect(ta_sb[:, entries]), ACT.Copy)
-                nc.vector.tensor_tensor(pa[:], pra[:], weight, ALU.mult)
-            else:
-                nc.vector.tensor_tensor(pa[:], prec[t][:].indirect(ta_sb[:, entries]), weight, ALU.mult)
+            nc.vector.tensor_tensor(pa[:], prec_neg[t][:].indirect(ta_sb[:, entries]), weight, ALU.mult)
             pb = work.tile([P, width], F32, name="pb")
-            nc.vector.scalar_tensor_tensor(pb[:], weight, 1.0, prb_neg[:], ALU.subtract, ALU.mult)
+            nc.vector.scalar_tensor_tensor(pb[:], weight, 1.0, prb[:], ALU.subtract, ALU.mult)
             na = work.tile([P, width], F32, name="na")
             nc.vector.tensor_tensor(na[:], mean[t][:].indirect(ta_sb[:, entries]), pa[:], ALU.mult)
             nb = work.tile([P, width], F32, name="nb")
-            if n in BFUSED:
-                nc.vector.tensor_tensor(nb[:], mean[t][:].indirect(tb_sb[:, entries]), pb[:], ALU.mult)
-            else:
-                nc.vector.tensor_tensor(nb[:], yb[:], pb[:], ALU.mult)
+            nc.vector.tensor_tensor(nb[:], yb[:], pb[:], ALU.mult)
             return pa, pb, na, nb
 
         def turn_and_add(name, width, left, right):
@@ -224,29 +195,22 @@ def tile_picked_ycovin_mean_p_kernel(
                         stop=(n == 1),
                         is_transpose=True,
                     )
-            return acc[:, 0:width].rearrange("r (q u e) -> r u q e", u=2, e=2)
+            return acc[:, 0:width].rearrange("r (m u e) -> r u m e", u=2, e=2)
 
-        hid_rows = keep.tile([P, BLOCKS, 2, HALF], BF16, name="hid_rows")
+        hid_rows = keep.tile([P, U // P, 2, HALF], BF16, name="hid_rows")
 
-        def divide(n, t, first, width, den, num):
-            planes = "r (u q e) -> r u q e"
+        def divide(t, first, width, den, num):
+            walk = "r (u m e) -> r u m e"
             root = work.tile([P, width], F32, name="root")
-            nc.scalar.activation(root[:].rearrange(planes, u=2, e=2), den, ACT.Abs_reciprocal_sqrt)
+            nc.scalar.activation(root[:].rearrange(walk, u=2, e=2), den, ACT.Abs_reciprocal_sqrt)
             sign = work.tile([P, width], BF16, name="sign")
+            nc.scalar.activation(sign[:].rearrange(walk, u=2, e=2), den, ACT.Sign)
             inverse = work.tile([P, width], F32, name="inverse")
+            nc.scalar.activation(inverse[:], root[:], ACT.Square)
             unsigned = work.tile([P, width], BF16, name="unsigned")
-            if n in VSQ:
-                nc.scalar.activation(sign[:].rearrange(planes, u=2, e=2), den, ACT.Sign)
-                nc.vector.tensor_tensor(
-                    inverse[:].rearrange(planes, u=2, e=2), num, root[:].rearrange(planes, u=2, e=2), ALU.mult
-                )
-                nc.vector.tensor_tensor(unsigned[:], inverse[:], root[:], ALU.mult)
-            else:
-                nc.scalar.activation(sign[:].rearrange(planes, u=2, e=2), den, ACT.Sign)
-                nc.scalar.activation(inverse[:], root[:], ACT.Square)
-                nc.vector.tensor_tensor(
-                    unsigned[:].rearrange(planes, u=2, e=2), num, inverse[:].rearrange(planes, u=2, e=2), ALU.mult
-                )
+            nc.vector.tensor_tensor(
+                unsigned[:].rearrange(walk, u=2, e=2), num, inverse[:].rearrange(walk, u=2, e=2), ALU.mult
+            )
             run = P // 2
             target = hid_rows[:, first // P : (first + width) // P, :, t * run : (t + 1) * run]
             nc.vector.tensor_tensor(
@@ -262,17 +226,17 @@ def tile_picked_ycovin_mean_p_kernel(
             for b in range(blocks):
                 for u in range(2):
                     at = (2 * b + u) * P
-                    words = hid_rows[:, first // P + b, u, :].bitcast(F32)
-                    nc.tensor.transpose(acc[:, at : at + P], words, ident[:])
-            grouped = work.tile([P, width, PACK], BF16, name="hid_grouped", align_bytes=64)
+                    nc.tensor.transpose(acc[:, at : at + P], hid_rows[:, first // P + b, u, :].bitcast(F32), ident[:])
+            interleaved = work.tile([P, width, PACK], BF16, name="hid_interleaved", align_bytes=64)
+            words = interleaved[:].rearrange("p r j -> p (r j)").bitcast(F32)
             nc.scalar.copy(
-                out=grouped[:].rearrange("p r j -> p (r j)").bitcast(F32).rearrange("p (b r u) -> p b r u", b=blocks, u=2),
+                out=words.rearrange("p (b r u) -> p b r u", b=blocks, u=2),
                 in_=acc[:, 0 : 2 * width].rearrange("p (b u r) -> p b r u", b=blocks, u=2),
             )
-            return grouped
+            return interleaved
 
-        def last_layer(first, width, grouped, copy):
-            codes, scales = quantize(work, "hid", grouped)
+        def last_layer(first, width, interleaved):
+            codes, scales = quantize(work, "hid", interleaved)
             acc = bank("result")
             nc.tensor.matmul_mx(
                 out=acc[:, 0:width],
@@ -284,30 +248,31 @@ def tile_picked_ycovin_mean_p_kernel(
                 stop=True,
             )
             result = work.tile([P, width], F32, name="result_sb")
-            copy(result[:], acc[:, 0:width])
+            nc.scalar.copy(result[:], acc[:, 0:width])
             nc.sync.dma_start(out=out[:, first : first + width], in_=result[:])
 
         last = ROW_TILES - 1
         steps = [(t, 0, WIDE) for t in range(ROW_TILES)] + [(t, WIDE, WIDE) for t in range(last)]
         steps.extend((last, WIDE + sum(LAST_WIDTHS[0:n]), width) for n, width in enumerate(LAST_WIDTHS))
-        sums, whole, turned = {}, [], []
+
+        sums, complete, turned = {}, [], []
         for n in range(len(steps) + 3):
-            if n == 1:
-                means(1)
+            if n < 2:
+                means(n)
             if n == 2:
-                w3_codes, w3_scales = quantize(keep, "w3", round_and_interleave("w3", w3_raw))
+                w3_codes, w3_scales = quantize(keep, "w3", round_and_interleave("w3", w3_raw, 1.0, False))
             if n < len(steps):
-                pa, pb, na, nb = products(n, *steps[n])
+                pa, pb, na, nb = products(*steps[n])
             if turned:
-                last_layer(*turned.pop(0), nc.vector.tensor_copy if n in [] else nc.scalar.copy)
-            if whole:
-                first, width = whole.pop(0)
+                last_layer(*turned.pop(0))
+            if complete:
+                first, width = complete.pop(0)
                 turned.append((first, width, turn_back(first, width)))
-            if 0 <= n - 1 < len(steps):
+            if 1 <= n <= len(steps):
                 t, first, width = steps[n - 1]
-                divide(n - 1, t, first, width, *sums[n - 1])
+                divide(t, first, width, *sums[n - 1])
                 if t == last:
-                    whole.extend((at, min(width, HALF)) for at in range(first, first + width, HALF))
+                    complete.extend((at, min(width, TURN)) for at in range(first, first + width, TURN))
             if n < len(steps):
                 width = steps[n][2]
                 sums[n] = (turn_and_add("den", width, pa, pb), turn_and_add("num", width, na, nb))

import math
from contextlib import ExitStack

import concourse.mybir as mybir
from concourse.masks import make_identity

K, T, S, N, H, U = 1024, 1024, 512, 128, 512, 1024
FLOPS = 2 * (2 * K * H * S + H * N * U)

F32 = mybir.dt.float32
BF16 = mybir.dt.bfloat16
I32 = mybir.dt.int32
U32 = mybir.dt.uint32
U16 = mybir.dt.uint16
U8 = mybir.dt.uint8
FP8X4 = mybir.dt.float8_e4m3fn_x4
ALU = mybir.AluOpType
ACT = mybir.ActivationFunctionType

P = 128
PACK = 4
K_PASS = P * PACK
PASSES = K // K_PASS
QUADRANT = 32
SCALE_ROWS = 4
ROW_TILES = H // P
HALF = H // 2
BANK = 512
BANKS = 8
LIST_ROWS = 16
WINDOW = S + LIST_ROWS
WIDE = BANK
TURN = BANK // 2
LAST_WIDTHS = [256, 128, 128]
WORK_BUFS = 3
TINY = 1e-15


def tile_picked_ycovin_mean_p_kernel(
    tc, x_words, x_scales, w1, w2, om, unit, w3, offs, ta, tb, out
):
    nc = tc.nc
    with ExitStack() as ctx:
        keep = ctx.enter_context(tc.tile_pool(name="keep", bufs=1))
        work = ctx.enter_context(tc.tile_pool(name="work", bufs=WORK_BUFS))
        psum = ctx.enter_context(tc.psum_pool(name="psum", bufs=BANKS))

        def bank(name):
            return psum.tile([P, BANK], F32, name=name, tag="bank")

        def load_list(name, source):
            tile = keep.tile(list(source.shape), U16, name=name)
            nc.sync.dma_start(tile[:], source)
            return tile

        def load_words(o):
            tile = keep.tile([P, T], U32, name=f"word_table{o}", align_bytes=64)
            nc.sync.dma_start(out=tile[:].bitcast(I32), in_=x_words[o].rearrange("p n j -> p (n j)").bitcast(I32))
            return tile

        def load_rows(name, rows):
            tile = keep.tile([P, PACK, rows.shape[1]], F32, name=name + "_raw")
            nc.sync.dma_start(out=tile[:], in_=rows.rearrange("(p j) c -> p j c", j=PACK))
            return tile

        def load_piece(name, w, o, h):
            return load_rows(f"{name}_{o}{h}", w[o * K_PASS : (o + 1) * K_PASS, h * HALF : (h + 1) * HALF])

        def window(name):
            tile = keep.tile([P, WINDOW], F32, name=name)
            nc.gpsimd.memset(tile[:, S:WINDOW], 0.0)
            return tile

        scale_table = keep.tile([P, T], U8, name="scale_table", align_bytes=64)
        nc.gpsimd.memset(scale_table[:].bitcast(I32), 0)
        ident = keep.tile([P, P], F32, name="ident")
        make_identity(nc, ident[:])
        prec_neg = [window(f"prec_neg{t}") for t in range(ROW_TILES)]
        mean = [window(f"mean{t}") for t in range(ROW_TILES)]

        offs_sb = load_list("offs_sb", offs)
        word_tables = [load_words(0)]
        for q in range(P // QUADRANT):
            nc.sync.dma_start(
                out=scale_table[QUADRANT * q : QUADRANT * q + SCALE_ROWS * PASSES, :].bitcast(I32),
                in_=x_scales.bitcast(I32)[:, SCALE_ROWS * q : SCALE_ROWS * (q + 1), :],
            )
        w2_raw = {(0, 0): load_piece("w2", w2, 0, 0)}
        word_tables.append(load_words(1))
        for o, h in ((1, 0), (0, 1), (1, 1)):
            w2_raw[o, h] = load_piece("w2", w2, o, h)
        w1_raw = {(o, 0): load_piece("w1", w1, o, 0) for o in range(PASSES)}
        unit_sb = keep.tile([P, ROW_TILES], F32, name="unit_sb")
        with nc.allow_non_contiguous_dma(reason="one value a partition and row tile"):
            nc.sync.dma_start(out=unit_sb[:], in_=unit.rearrange("(t p) one -> p (t one)", p=P))
        ta_sb = load_list("ta_sb", ta)
        tb_sb = load_list("tb_sb", tb)
        for o in range(PASSES):
            w1_raw[o, 1] = load_piece("w1", w1, o, 1)
        om_sb = []
        for t in range(ROW_TILES):
            om_sb.append(keep.tile([P, U], F32, name=f"om{t}"))
            nc.sync.dma_start(out=om_sb[t][:], in_=om[t * P : (t + 1) * P, :])
        w3_raw = load_rows("w3", w3)

        x_codes = []
        for o in range(PASSES):
            x_codes.append(keep.tile([P, S], U32, name=f"x_codes{o}", align_bytes=64))
            nc.vector.tensor_copy(x_codes[o][:], word_tables[o][:].indirect(offs_sb[:]))
        x_scale = keep.tile([P, S], U8, name="x_scale", align_bytes=64)
        nc.vector.tensor_copy(x_scale[:], scale_table[:].indirect(offs_sb[:]))

        def round_and_interleave(name, raw, factor, on_scalar):
            tile = keep.tile([P, raw.shape[2], PACK], BF16, name=name + "_bf16", align_bytes=64)
            target = tile[:].rearrange("p (c i) j -> p c j i", i=4)
            source = raw[:].rearrange("p j (c i) -> p c j i", i=4)
            if on_scalar:
                nc.scalar.activation(target, source, ACT.Copy, scale=factor)
            else:
                nc.vector.tensor_scalar(target, source, factor, None, ALU.mult)
            return tile

        def quantize(pool, name, interleaved):
            columns = interleaved.shape[1]
            codes = pool.tile([P, columns], U32, name=name + "_codes", align_bytes=64)
            scales = pool.tile([P, columns], U8, name=name + "_scales", align_bytes=64)
            nc.vector.quantize_mx(
                out=codes[:].bitcast(FP8X4), scales=scales[:], in_=interleaved[:].rearrange("p c j -> p (c j)")
            )
            return codes, scales

        def first_layer(name, raw, h, factor, on_scalar):
            rounded = [round_and_interleave(f"{name}_{o}{h}", raw[o, h], factor, on_scalar) for o in range(PASSES)]
            packed = [quantize(keep, f"{name}_{o}{h}", rounded[o]) for o in range(PASSES)]
            banks = []
            for column in range(0, HALF, P):
                acc = bank(f"{name}_acc")
                for o, (codes, scales) in enumerate(packed):
                    nc.tensor.matmul_mx(
                        out=acc[:],
                        lhsT=codes[:, column : column + P].bitcast(FP8X4),
                        lhsT_scale=scales[:, column : column + P],
                        rhs=x_codes[o][:].bitcast(FP8X4),
                        rhs_scale=x_scale[SCALE_ROWS * o : P, :],
                        start=(o == 0),
                        stop=(o == PASSES - 1),
                    )
                banks.append(acc)
            return banks

        z = first_layer("w2", w2_raw, 0, -1.0, True) + first_layer("w2", w2_raw, 1, -1.0, False)

        slot = [0, 2, 3, 1]
        sigmoid = keep.tile([P, ROW_TILES, S], F32, name="sigmoid")
        for t in range(ROW_TILES):
            nc.scalar.activation(sigmoid[:, slot[t], :], z[t][:], ACT.Sigmoid)
        outer_logs = keep.tile([P, 2, S], F32, name="outer_logs")
        nc.scalar.activation(outer_logs[:], sigmoid[:, 0:2, :], ACT.Ln, bias=TINY, scale=math.exp(-0.5))
        inner_logs = sigmoid[:, 0:2, :]
        nc.scalar.activation(inner_logs, sigmoid[:, 2:4, :], ACT.Ln, bias=TINY, scale=math.exp(-0.5))
        logs = [outer_logs[:, 0, :], inner_logs[:, 0, :], inner_logs[:, 1, :], outer_logs[:, 1, :]]
        for t in range(ROW_TILES):
            nc.vector.scalar_tensor_tensor(prec_neg[t][:, 0:S], z[t][:], -0.5, logs[t], ALU.add, ALU.min)

        def means(h):
            for t, acc in enumerate(first_layer("w1", w1_raw, h, 1.0, False), start=2 * h):
                nc.scalar.activation(mean[t][:, 0:S], acc[:], ACT.Copy, scale=unit_sb[:, t : t + 1])

        def products(t, first, width):
            entries = slice(first // LIST_ROWS, (first + width) // LIST_ROWS)
            weight = om_sb[t][:, first : first + width]
            prb = work.tile([P, width], F32, name="prb")
            nc.scalar.activation(prb[:], prec_neg[t][:].indirect(tb_sb[:, entries]), ACT.Copy, scale=-1.0)
            yb = work.tile([P, width], F32, name="yb", bufs=WORK_BUFS + 1)
            nc.scalar.activation(yb[:], mean[t][:].indirect(tb_sb[:, entries]), ACT.Copy)
            pa = work.tile([P, width], F32, name="pa")
            nc.vector.tensor_tensor(pa[:], prec_neg[t][:].indirect(ta_sb[:, entries]), weight, ALU.mult)
            pb = work.tile([P, width], F32, name="pb")
            nc.vector.scalar_tensor_tensor(pb[:], weight, 1.0, prb[:], ALU.subtract, ALU.mult)
            na = work.tile([P, width], F32, name="na")
            nc.vector.tensor_tensor(na[:], mean[t][:].indirect(ta_sb[:, entries]), pa[:], ALU.mult)
            nb = work.tile([P, width], F32, name="nb")
            nc.vector.tensor_tensor(nb[:], yb[:], pb[:], ALU.mult)
            return pa, pb, na, nb

        def turn_and_add(name, width, left, right):
            acc = bank(name)
            for at in range(0, width, P):
                for n, term in enumerate((left, right)):
                    nc.tensor.matmul(
                        acc[:, at : at + P],
                        lhsT=term[:, at : at + P],
                        rhs=ident[:],
                        start=(n == 0),
                        stop=(n == 1),
                        is_transpose=True,
                    )
            return acc[:, 0:width].rearrange("r (m u e) -> r u m e", u=2, e=2)

        hid_rows = keep.tile([P, U // P, 2, HALF], BF16, name="hid_rows")

        def divide(t, first, width, den, num):
            walk = "r (u m e) -> r u m e"
            root = work.tile([P, width], F32, name="root")
            nc.scalar.activation(root[:].rearrange(walk, u=2, e=2), den, ACT.Abs_reciprocal_sqrt)
            sign = work.tile([P, width], BF16, name="sign")
            nc.scalar.activation(sign[:].rearrange(walk, u=2, e=2), den, ACT.Sign)
            inverse = work.tile([P, width], F32, name="inverse")
            nc.scalar.activation(inverse[:], root[:], ACT.Square)
            unsigned = work.tile([P, width], BF16, name="unsigned")
            nc.vector.tensor_tensor(
                unsigned[:].rearrange(walk, u=2, e=2), num, inverse[:].rearrange(walk, u=2, e=2), ALU.mult
            )
            run = P // 2
            target = hid_rows[:, first // P : (first + width) // P, :, t * run : (t + 1) * run]
            nc.vector.tensor_tensor(
                target.rearrange("r b u c -> r u b c"),
                unsigned[:].rearrange("r (u b c) -> r u b c", u=2, c=run),
                sign[:].rearrange("r (u b c) -> r u b c", u=2, c=run),
                ALU.mult,
            )

        def turn_back(first, width):
            blocks = width // P
            acc = bank("turned")
            for b in range(blocks):
                for u in range(2):
                    at = (2 * b + u) * P
                    nc.tensor.transpose(acc[:, at : at + P], hid_rows[:, first // P + b, u, :].bitcast(F32), ident[:])
            interleaved = work.tile([P, width, PACK], BF16, name="hid_interleaved", align_bytes=64)
            words = interleaved[:].rearrange("p r j -> p (r j)").bitcast(F32)
            nc.scalar.copy(
                out=words.rearrange("p (b r u) -> p b r u", b=blocks, u=2),
                in_=acc[:, 0 : 2 * width].rearrange("p (b u r) -> p b r u", b=blocks, u=2),
            )
            return interleaved

        def last_layer(first, width, interleaved):
            codes, scales = quantize(work, "hid", interleaved)
            acc = bank("result")
            nc.tensor.matmul_mx(
                out=acc[:, 0:width],
                lhsT=w3_codes[:].bitcast(FP8X4),
                lhsT_scale=w3_scales[:],
                rhs=codes[:].bitcast(FP8X4),
                rhs_scale=scales[:],
                start=True,
                stop=True,
            )
            result = work.tile([P, width], F32, name="result_sb")
            nc.scalar.copy(result[:], acc[:, 0:width])
            nc.sync.dma_start(out=out[:, first : first + width], in_=result[:])

        last = ROW_TILES - 1
        steps = [(t, 0, WIDE) for t in range(ROW_TILES)] + [(t, WIDE, WIDE) for t in range(last)]
        steps.extend((last, WIDE + sum(LAST_WIDTHS[0:n]), width) for n, width in enumerate(LAST_WIDTHS))

        sums, complete, turned = {}, [], []
        for n in range(len(steps) + 3):
            if n < 2:
                means(n)
            if n == 2:
                w3_codes, w3_scales = quantize(keep, "w3", round_and_interleave("w3", w3_raw, 1.0, False))
            if n < len(steps):
                pa, pb, na, nb = products(*steps[n])
            if turned:
                last_layer(*turned.pop(0))
            if complete:
                first, width = complete.pop(0)
                turned.append((first, width, turn_back(first, width)))
            if 1 <= n <= len(steps):
                t, first, width = steps[n - 1]
                divide(t, first, width, *sums[n - 1])
                if t == last:
                    complete.extend((at, min(width, TURN)) for at in range(first, first + width, TURN))
            if n < len(steps):
                width = steps[n][2]
                sums[n] = (turn_and_add("den", width, pa, pb), turn_and_add("num", width, na, nb))
